import numpy as np
import ml_dtypes


def mxq(x, axis, fmt="e4m3"):
    dtype, down = {"e4m3": (ml_dtypes.float8_e4m3fn, 7), "e5m2": (ml_dtypes.float8_e5m2, 14)}[fmt]
    v = np.moveaxis(np.asarray(x, np.float32).astype(ml_dtypes.bfloat16).astype(np.float64), axis, -1)
    blocks = v.reshape(v.shape[:-1] + (-1, 32))
    amax = np.abs(blocks).max(-1, keepdims=True)
    byte = np.maximum(np.where(amax > 0, np.frexp(amax)[1] - 1 + 127, 0) - down, 1)
    scale = np.exp2(byte - 127.0)
    codes = (blocks / scale).astype(np.float32).astype(dtype).astype(np.float64)
    return np.moveaxis((codes * scale).reshape(v.shape), -1, axis)


WIDE = False


def mx_kscale(k):
    if not WIDE:
        return np.ones(k)
    levels = np.array([10, -10, 5, -5, 0])
    if k % 512:
        return np.exp2(np.random.permutation(np.resize(levels, k // 32))).repeat(32)
    a = np.empty((k // 512, 16))
    for p in range(k // 512):
        a[p, :8] = np.random.permutation(np.resize(levels, 8))
        for g in range(8):
            far = levels[np.abs(levels - a[p, g]) >= 10]
            a[p, g + 8] = far[np.random.randint(len(far))]
    return np.exp2(a.ravel()).repeat(32)


def f64(x):
    return np.asarray(x).astype(np.float64)


def striped(idx):
    return np.tile(idx.reshape(-1, 16).T, (8, 1)).astype(np.uint16)


def unstriped(offs):
    return offs[:16].T.reshape(-1).astype(np.int64)


def gelu(v):
    return 0.5 * v * (1.0 + np.tanh(np.sqrt(2.0 / np.pi) * (v + 0.044715 * v**3)))


K, T, S, V, N = 512, 2048, 512, 512, 1024


def setup_inputs():
    n = np.random.standard_normal
    s = mx_kscale(K)[:, None]
    return {
        "xT": (n((K, T)) * s).astype(np.float32),
        "w": (n((K, N)) / np.sqrt(K) / s).astype(np.float32),
        "b": (0.3 * n((V, 1))).astype(np.float32),
        "offs": striped(np.random.permutation(T)[:S]),
        "pos1": striped(np.random.permutation(N)[:V]),
    }


def reference(xT, w, b, offs, pos1):
    y = mxq(f64(w)[:, unstriped(pos1)], 0, "e4m3").T @ mxq(f64(xT)[:, unstriped(offs)], 0, "e4m3")
    return gelu(y + f64(b))

@@ -1,0 +1,105 @@
+from contextlib import ExitStack
+
+import concourse.mybir as mybir
+
+K, T, S, V, N = 512, 2048, 512, 512, 1024
+FLOPS = 2 * K * S * V
+
+F32 = mybir.dt.float32
+BF16 = mybir.dt.bfloat16
+U32 = mybir.dt.uint32
+U16 = mybir.dt.uint16
+U8 = mybir.dt.uint8
+FP8X4 = mybir.dt.float8_e4m3fn_x4
+COPY = mybir.ActivationFunctionType.Copy
+GELU = mybir.ActivationFunctionType.Gelu_apprx_tanh
+
+P = 128
+PACK = 4
+LIST_ROWS = 16
+W_TILES = V // P
+TOKENS = 256
+X_SLICES = S // TOKENS
+
+
+def tile_picked_cross_gelu_l_kernel(tc, xT, w, b, offs, pos1, out):
+    nc = tc.nc
+    x_planes = xT.rearrange("(p t) c -> p t c", t=PACK)
+    w_planes = w.rearrange("(p t) c -> p t c", t=PACK)
+
+    with ExitStack() as ctx:
+        keep = ctx.enter_context(tc.tile_pool(name="keep", bufs=1))
+        psum = ctx.enter_context(tc.psum_pool(name="psum", bufs=1))
+
+        warm = keep.tile([P, 8], F32, name="warm")
+        nc.vector.memset(warm[:], 0.0)
+        warm_out = keep.tile([P, 8], F32, name="warm_out")
+        nc.scalar.activation(warm_out[:], warm[:], GELU)
+
+        pos1_sb = keep.tile([P, V // LIST_ROWS], U16, name="pos1_sb")
+        offs_sb = keep.tile([P, S // LIST_ROWS], U16, name="offs_sb")
+        w_sb = [keep.tile([P, N], F32, name=f"w{t}") for t in range(PACK)]
+        x_sb = [keep.tile([P, T], F32, name=f"x{t}") for t in range(PACK)]
+        b_sb = keep.tile([P, W_TILES], F32, name="b_sb")
+        nc.sync.dma_start(pos1_sb[:], pos1)
+        for t in range(PACK):
+            nc.sync.dma_start(w_sb[t][:], w_planes[:, t, :])
+        nc.sync.dma_start(offs_sb[:], offs)
+        for t in range(PACK):
+            nc.sync.dma_start(x_sb[t][:], x_planes[:, t, :])
+        with nc.allow_non_contiguous_dma(reason="one bias a partition"):
+            nc.sync.dma_start(b_sb[:], b.rearrange("(m p) o -> p (m o)", p=P))
+
+        w_got = keep.tile([P, PACK, V], F32, name="w_got")
+        for t in range(PACK):
+            nc.vector.tensor_copy(w_got[:, t, :], w_sb[t][:].indirect(pos1_sb[:]))
+        w_grouped = keep.tile([P, V, PACK], BF16, name="w_grouped", align_bytes=64)
+        w_codes = keep.tile([P, V], U32, name="w_codes", align_bytes=64)
+        w_scales = keep.tile([P, V], U8, name="w_scales", align_bytes=64)
+        for m in range(W_TILES):
+            cols = slice(m * P, (m + 1) * P)
+            nc.scalar.copy(w_grouped[:, cols, :], w_got[:, :, cols].rearrange("p t n -> p n t"))
+        for m in range(W_TILES):
+            cols = slice(m * P, (m + 1) * P)
+            nc.vector.quantize_mx(
+                out=w_codes[:, cols].bitcast(FP8X4),
+                scales=w_scales[:, cols],
+                in_=w_grouped[:, cols, :].rearrange("p n t -> p (n t)"),
+            )
+
+        x_grouped = [keep.tile([P, TOKENS, PACK], BF16, name=f"xg{s}", align_bytes=64) for s in range(X_SLICES)]
+        x_codes = [keep.tile([P, TOKENS], U32, name=f"xc{s}", align_bytes=64) for s in range(X_SLICES)]
+        x_scales = [keep.tile([P, TOKENS], U8, name=f"xs{s}", align_bytes=64) for s in range(X_SLICES)]
+        list_cols = TOKENS // LIST_ROWS
+
+        def gather_tokens(t, s):
+            nc.vector.tensor_copy(
+                x_grouped[s][:, :, t],
+                x_sb[t][:].indirect(offs_sb[:, s * list_cols : (s + 1) * list_cols]),
+            )
+
+        for t in range(PACK - 1):
+            for s in range(X_SLICES):
+                gather_tokens(t, s)
+        for s in range(X_SLICES):
+            gather_tokens(PACK - 1, s)
+            nc.vector.quantize_mx(
+                out=x_codes[s][:].bitcast(FP8X4),
+                scales=x_scales[s][:],
+                in_=x_grouped[s][:].rearrange("p n t -> p (n t)"),
+            )
+            for m in range(W_TILES):
+                cols = slice(m * P, (m + 1) * P)
+                acc = psum.tile([P, TOKENS], F32, name=f"acc{s}_{m}")
+                nc.tensor.matmul_mx(
+                    out=acc[:],
+                    lhsT=w_codes[:, cols].bitcast(FP8X4),
+                    lhsT_scale=w_scales[:, cols],
+                    rhs=x_codes[s][:].bitcast(FP8X4),
+                    rhs_scale=x_scales[s][:],
+                    start=True,
+                    stop=True,
+                )
+                res = keep.tile([P, TOKENS], F32, name=f"res{s}_{m}")
+                nc.scalar.activation(res[:], acc[:], GELU, bias=b_sb[:, m : m + 1])
+                nc.sync.dma_start(out[cols, s * TOKENS : (s + 1) * TOKENS], res[:])

@@ -1,6 +1,7 @@
 from contextlib import ExitStack
 
 import concourse.mybir as mybir
+from concourse.masks import make_identity
 
 K, T, S, V, N = 512, 2048, 512, 512, 1024
 FLOPS = 2 * K * S * V
@@ -11,7 +12,6 @@ U32 = mybir.dt.uint32
 U16 = mybir.dt.uint16
 U8 = mybir.dt.uint8
 FP8X4 = mybir.dt.float8_e4m3fn_x4
-COPY = mybir.ActivationFunctionType.Copy
 GELU = mybir.ActivationFunctionType.Gelu_apprx_tanh
 
 P = 128
@@ -40,15 +40,22 @@ def tile_picked_cross_gelu_l_kernel(tc, xT, w, b, offs, pos1, out):
         offs_sb = keep.tile([P, S // LIST_ROWS], U16, name="offs_sb")
         w_sb = [keep.tile([P, N], F32, name=f"w{t}") for t in range(PACK)]
         x_sb = [keep.tile([P, T], F32, name=f"x{t}") for t in range(PACK)]
-        b_sb = keep.tile([P, W_TILES], F32, name="b_sb")
+        b_rows = keep.tile([P, P], F32, name="b_rows")
+        nc.vector.memset(b_rows[:], 0.0)
+        ident = keep.tile([P, P], F32, name="ident")
+        make_identity(nc, ident[:])
         nc.sync.dma_start(pos1_sb[:], pos1)
         for t in range(PACK):
             nc.sync.dma_start(w_sb[t][:], w_planes[:, t, :])
         nc.sync.dma_start(offs_sb[:], offs)
+        nc.sync.dma_start(b_rows[0:W_TILES, :], b.rearrange("(m p) o -> m (p o)", p=P))
         for t in range(PACK):
             nc.sync.dma_start(x_sb[t][:], x_planes[:, t, :])
-        with nc.allow_non_contiguous_dma(reason="one bias a partition"):
-            nc.sync.dma_start(b_sb[:], b.rearrange("(m p) o -> p (m o)", p=P))
+
+        b_turned = psum.tile([P, TOKENS], F32, name="acc1_3")
+        nc.tensor.transpose(b_turned[:, 0:P], b_rows[:], ident[:])
+        b_sb = keep.tile([P, W_TILES], F32, name="b_sb")
+        nc.vector.tensor_copy(b_sb[:], b_turned[:, 0:W_TILES])
 
         w_got = keep.tile([P, PACK, V], F32, name="w_got")
         for t in range(PACK):
@@ -67,26 +74,25 @@ def tile_picked_cross_gelu_l_kernel(tc, xT, w, b, offs, pos1, out):
                 in_=w_grouped[:, cols, :].rearrange("p n t -> p (n t)"),
             )
 
-        x_grouped = [keep.tile([P, TOKENS, PACK], BF16, name=f"xg{s}", align_bytes=64) for s in range(X_SLICES)]
-        x_codes = [keep.tile([P, TOKENS], U32, name=f"xc{s}", align_bytes=64) for s in range(X_SLICES)]
-        x_scales = [keep.tile([P, TOKENS], U8, name=f"xs{s}", align_bytes=64) for s in range(X_SLICES)]
-        list_cols = TOKENS // LIST_ROWS
-
-        def gather_tokens(t, s):
-            nc.vector.tensor_copy(
-                x_grouped[s][:, :, t],
-                x_sb[t][:].indirect(offs_sb[:, s * list_cols : (s + 1) * list_cols]),
-            )
+        x_grouped = keep.tile([P, S, PACK], BF16, name="x_grouped", align_bytes=64)
+        x_codes = keep.tile([P, S], U32, name="x_codes", align_bytes=64)
+        x_scales = keep.tile([P, S], U8, name="x_scales", align_bytes=64)
 
         for t in range(PACK - 1):
-            for s in range(X_SLICES):
-                gather_tokens(t, s)
+            nc.vector.tensor_copy(x_grouped[:, :, t], x_sb[t][:].indirect(offs_sb[:]))
         for s in range(X_SLICES):
-            gather_tokens(PACK - 1, s)
+            toks = slice(s * TOKENS, (s + 1) * TOKENS)
+            entries = slice(s * TOKENS // LIST_ROWS, (s + 1) * TOKENS // LIST_ROWS)
+            nc.vector.tensor_copy(x_grouped[:, toks, PACK - 1], x_sb[PACK - 1][:].indirect(offs_sb[:, entries]))
+            if s + 1 < X_SLICES:
+                nc.gpsimd.tensor_copy(
+                    x_grouped[:, (s + 1) * TOKENS : (s + 1) * TOKENS + 2, PACK - 1],
+                    x_grouped[:, s * TOKENS : s * TOKENS + 2, PACK - 1],
+                )
             nc.vector.quantize_mx(
-                out=x_codes[s][:].bitcast(FP8X4),
-                scales=x_scales[s][:],
-                in_=x_grouped[s][:].rearrange("p n t -> p (n t)"),
+                out=x_codes[:, toks].bitcast(FP8X4),
+                scales=x_scales[:, toks],
+                in_=x_grouped[:, toks, :].rearrange("p n t -> p (n t)"),
             )
             for m in range(W_TILES):
                 cols = slice(m * P, (m + 1) * P)
@@ -95,11 +101,11 @@ def tile_picked_cross_gelu_l_kernel(tc, xT, w, b, offs, pos1, out):
                     out=acc[:],
                     lhsT=w_codes[:, cols].bitcast(FP8X4),
                     lhsT_scale=w_scales[:, cols],
-                    rhs=x_codes[s][:].bitcast(FP8X4),
-                    rhs_scale=x_scales[s][:],
+                    rhs=x_codes[:, toks].bitcast(FP8X4),
+                    rhs_scale=x_scales[:, toks],
                     start=True,
                     stop=True,
                 )
                 res = keep.tile([P, TOKENS], F32, name=f"res{s}_{m}")
                 nc.scalar.activation(res[:], acc[:], GELU, bias=b_sb[:, m : m + 1])
-                nc.sync.dma_start(out[cols, s * TOKENS : (s + 1) * TOKENS], res[:])
+                nc.sync.dma_start(out[cols, toks], res[:])

@@ -38,7 +38,7 @@ def tile_picked_cross_gelu_l_kernel(tc, xT, w, b, offs, pos1, out):
 
         pos1_sb = keep.tile([P, V // LIST_ROWS], U16, name="pos1_sb")
         offs_sb = keep.tile([P, S // LIST_ROWS], U16, name="offs_sb")
-        w_sb = [keep.tile([P, N], F32, name=f"w{t}") for t in range(PACK)]
+        w_sb = [keep.tile([P, 2, N], F32, name=f"w{u}") for u in range(2)]
         x_sb = [keep.tile([P, T], F32, name=f"x{t}") for t in range(PACK)]
         b_rows = keep.tile([P, P], F32, name="b_rows")
         nc.vector.memset(b_rows[:], 0.0)
@@ -46,7 +46,7 @@ def tile_picked_cross_gelu_l_kernel(tc, xT, w, b, offs, pos1, out):
         make_identity(nc, ident[:])
         nc.sync.dma_start(pos1_sb[:], pos1)
         for t in range(PACK):
-            nc.sync.dma_start(w_sb[t][:], w_planes[:, t, :])
+            nc.sync.dma_start(w_sb[t // 2][:, t % 2, :], w_planes[:, t, :])
         nc.sync.dma_start(offs_sb[:], offs)
         nc.sync.dma_start(b_rows[0:W_TILES, :], b.rearrange("(m p) o -> m (p o)", p=P))
         for t in range(PACK):
@@ -57,15 +57,17 @@ def tile_picked_cross_gelu_l_kernel(tc, xT, w, b, offs, pos1, out):
         b_sb = keep.tile([P, W_TILES], F32, name="b_sb")
         nc.vector.tensor_copy(b_sb[:], b_turned[:, 0:W_TILES])
 
-        w_got = keep.tile([P, PACK, V], F32, name="w_got")
-        for t in range(PACK):
-            nc.vector.tensor_copy(w_got[:, t, :], w_sb[t][:].indirect(pos1_sb[:]))
         w_grouped = keep.tile([P, V, PACK], BF16, name="w_grouped", align_bytes=64)
+        w_words = w_grouped[:].rearrange("p n t -> p (n t)").bitcast(U32).rearrange("p (n u) -> p n u", u=2)
         w_codes = keep.tile([P, V], U32, name="w_codes", align_bytes=64)
         w_scales = keep.tile([P, V], U8, name="w_scales", align_bytes=64)
-        for m in range(W_TILES):
-            cols = slice(m * P, (m + 1) * P)
-            nc.scalar.copy(w_grouped[:, cols, :], w_got[:, :, cols].rearrange("p t n -> p n t"))
+        for u in range(2):
+            w_pair = keep.tile([P, N, 2], BF16, name=f"w_pair{u}", align_bytes=64)
+            nc.scalar.copy(w_pair[:], w_sb[u][:].rearrange("p e c -> p c e"))
+            nc.vector.tensor_copy(
+                w_words[:, :, u],
+                w_pair[:].rearrange("p c e -> p (c e)").bitcast(U32).indirect(pos1_sb[:]),
+            )
         for m in range(W_TILES):
             cols = slice(m * P, (m + 1) * P)
             nc.vector.quantize_mx(
@@ -78,8 +80,11 @@ def tile_picked_cross_gelu_l_kernel(tc, xT, w, b, offs, pos1, out):
         x_codes = keep.tile([P, S], U32, name="x_codes", align_bytes=64)
         x_scales = keep.tile([P, S], U8, name="x_scales", align_bytes=64)
 
-        for t in range(PACK - 1):
-            nc.vector.tensor_copy(x_grouped[:, :, t], x_sb[t][:].indirect(offs_sb[:]))
+        x_got = keep.tile([P, 2, S], F32, name="x_got")
+        for t in range(2):
+            nc.vector.tensor_copy(x_got[:, t, :], x_sb[t][:].indirect(offs_sb[:]))
+        nc.scalar.copy(x_grouped[:, :, 0:2], x_got[:].rearrange("p t n -> p n t"))
+        nc.vector.tensor_copy(x_grouped[:, :, 2], x_sb[2][:].indirect(offs_sb[:]))
         for s in range(X_SLICES):
             toks = slice(s * TOKENS, (s + 1) * TOKENS)
             entries = slice(s * TOKENS // LIST_ROWS, (s + 1) * TOKENS // LIST_ROWS)

@@ -44,15 +44,15 @@ def tile_picked_cross_gelu_l_kernel(tc, xT, w, b, offs, pos1, out):
         nc.vector.memset(b_rows[:], 0.0)
         ident = keep.tile([P, P], F32, name="ident")
         make_identity(nc, ident[:])
+        nc.sync.dma_start(w_sb[0][:], w_planes[:, 0:2, :])
         nc.sync.dma_start(pos1_sb[:], pos1)
-        for t in range(PACK):
-            nc.sync.dma_start(w_sb[t // 2][:, t % 2, :], w_planes[:, t, :])
+        nc.sync.dma_start(w_sb[1][:], w_planes[:, 2:4, :])
         nc.sync.dma_start(offs_sb[:], offs)
         nc.sync.dma_start(b_rows[0:W_TILES, :], b.rearrange("(m p) o -> m (p o)", p=P))
         for t in range(PACK):
             nc.sync.dma_start(x_sb[t][:], x_planes[:, t, :])
 
-        b_turned = psum.tile([P, TOKENS], F32, name="acc1_3")
+        b_turned = psum.tile([P, TOKENS], F32, name="acc7")
         nc.tensor.transpose(b_turned[:, 0:P], b_rows[:], ident[:])
         b_sb = keep.tile([P, W_TILES], F32, name="b_sb")
         nc.vector.tensor_copy(b_sb[:], b_turned[:, 0:W_TILES])
@@ -80,6 +80,7 @@ def tile_picked_cross_gelu_l_kernel(tc, xT, w, b, offs, pos1, out):
         x_codes = keep.tile([P, S], U32, name="x_codes", align_bytes=64)
         x_scales = keep.tile([P, S], U8, name="x_scales", align_bytes=64)
 
+        banks = [1, 0, 7, 6, 5, 4, 3, 2, 1, 0]
         x_got = keep.tile([P, 2, S], F32, name="x_got")
         for t in range(2):
             nc.vector.tensor_copy(x_got[:, t, :], x_sb[t][:].indirect(offs_sb[:]))
@@ -94,23 +95,28 @@ def tile_picked_cross_gelu_l_kernel(tc, xT, w, b, offs, pos1, out):
                     x_grouped[:, (s + 1) * TOKENS : (s + 1) * TOKENS + 2, PACK - 1],
                     x_grouped[:, s * TOKENS : s * TOKENS + 2, PACK - 1],
                 )
-            nc.vector.quantize_mx(
-                out=x_codes[:, toks].bitcast(FP8X4),
-                scales=x_scales[:, toks],
-                in_=x_grouped[:, toks, :].rearrange("p n t -> p (n t)"),
-            )
-            for m in range(W_TILES):
-                cols = slice(m * P, (m + 1) * P)
-                acc = psum.tile([P, TOKENS], F32, name=f"acc{s}_{m}")
-                nc.tensor.matmul_mx(
-                    out=acc[:],
-                    lhsT=w_codes[:, cols].bitcast(FP8X4),
-                    lhsT_scale=w_scales[:, cols],
-                    rhs=x_codes[:, toks].bitcast(FP8X4),
-                    rhs_scale=x_scales[:, toks],
-                    start=True,
-                    stop=True,
+            for c0 in (toks.start, toks.start + P):
+                part = slice(c0, c0 + P)
+                nc.vector.quantize_mx(
+                    out=x_codes[:, part].bitcast(FP8X4),
+                    scales=x_scales[:, part],
+                    in_=x_grouped[:, part, :].rearrange("p n t -> p (n t)"),
                 )
+            for m in range(W_TILES):
+                words = slice(m * P, (m + 1) * P)
                 res = keep.tile([P, TOKENS], F32, name=f"res{s}_{m}")
-                nc.scalar.activation(res[:], acc[:], GELU, bias=b_sb[:, m : m + 1])
-                nc.sync.dma_start(out[cols, toks], res[:])
+                for c0 in range(0, TOKENS, P if m == 0 else TOKENS):
+                    width = P if m == 0 else TOKENS
+                    part = slice(toks.start + c0, toks.start + c0 + width)
+                    acc = psum.tile([P, TOKENS], F32, name=f"acc{banks.pop()}")
+                    nc.tensor.matmul_mx(
+                        out=acc[:, 0:width],
+                        lhsT=w_codes[:, words].bitcast(FP8X4),
+                        lhsT_scale=w_scales[:, words],
+                        rhs=x_codes[:, part].bitcast(FP8X4),
+                        rhs_scale=x_scales[:, part],
+                        start=True,
+                        stop=True,
+                    )
+                    nc.scalar.activation(res[:, c0 : c0 + width], acc[:, 0:width], GELU, bias=b_sb[:, m : m + 1])
+                nc.sync.dma_start(out[words, toks], res[:])

from contextlib import ExitStack

import concourse.mybir as mybir
from concourse.masks import make_identity

K, T, S, V, N = 512, 2048, 512, 512, 1024
FLOPS = 2 * K * S * V

F32 = mybir.dt.float32
BF16 = mybir.dt.bfloat16
U32 = mybir.dt.uint32
U16 = mybir.dt.uint16
U8 = mybir.dt.uint8
FP8X4 = mybir.dt.float8_e4m3fn_x4
GELU = mybir.ActivationFunctionType.Gelu_apprx_tanh

P = 128
PACK = 4
LIST_ROWS = 16
W_TILES = V // P
TOKENS = 256
X_SLICES = S // TOKENS


def tile_picked_cross_gelu_l_kernel(tc, xT, w, b, offs, pos1, out):
    nc = tc.nc
    x_planes = xT.rearrange("(p t) c -> p t c", t=PACK)
    w_planes = w.rearrange("(p t) c -> p t c", t=PACK)

    with ExitStack() as ctx:
        keep = ctx.enter_context(tc.tile_pool(name="keep", bufs=1))
        psum = ctx.enter_context(tc.psum_pool(name="psum", bufs=1))

        warm = keep.tile([P, 8], F32, name="warm")
        nc.vector.memset(warm[:], 0.0)
        warm_out = keep.tile([P, 8], F32, name="warm_out")
        nc.scalar.activation(warm_out[:], warm[:], GELU)

        pos1_sb = keep.tile([P, V // LIST_ROWS], U16, name="pos1_sb")
        offs_sb = keep.tile([P, S // LIST_ROWS], U16, name="offs_sb")
        w_sb = [keep.tile([P, 2, N], F32, name=f"w{u}") for u in range(2)]
        x_sb = [keep.tile([P, T], F32, name=f"x{t}") for t in range(PACK)]
        b_rows = keep.tile([P, P], F32, name="b_rows")
        nc.vector.memset(b_rows[:], 0.0)
        ident = keep.tile([P, P], F32, name="ident")
        make_identity(nc, ident[:])
        nc.sync.dma_start(w_sb[0][:], w_planes[:, 0:2, :])
        nc.sync.dma_start(pos1_sb[:], pos1)
        nc.sync.dma_start(w_sb[1][:], w_planes[:, 2:4, :])
        nc.sync.dma_start(offs_sb[:], offs)
        nc.sync.dma_start(b_rows[0:W_TILES, :], b.rearrange("(m p) o -> m (p o)", p=P))
        for t in range(PACK):
            nc.sync.dma_start(x_sb[t][:], x_planes[:, t, :])

        b_turned = psum.tile([P, TOKENS], F32, name="acc7")
        nc.tensor.transpose(b_turned[:, 0:P], b_rows[:], ident[:])
        b_sb = keep.tile([P, W_TILES], F32, name="b_sb")
        nc.vector.tensor_copy(b_sb[:], b_turned[:, 0:W_TILES])

        w_grouped = keep.tile([P, V, PACK], BF16, name="w_grouped", align_bytes=64)
        w_words = w_grouped[:].rearrange("p n t -> p (n t)").bitcast(U32).rearrange("p (n u) -> p n u", u=2)
        w_codes = keep.tile([P, V], U32, name="w_codes", align_bytes=64)
        w_scales = keep.tile([P, V], U8, name="w_scales", align_bytes=64)
        for u in range(2):
            w_pair = keep.tile([P, N, 2], BF16, name=f"w_pair{u}", align_bytes=64)
            nc.scalar.copy(w_pair[:], w_sb[u][:].rearrange("p e c -> p c e"))
            nc.vector.tensor_copy(
                w_words[:, :, u],
                w_pair[:].rearrange("p c e -> p (c e)").bitcast(U32).indirect(pos1_sb[:]),
            )
        for m in range(W_TILES):
            cols = slice(m * P, (m + 1) * P)
            nc.vector.quantize_mx(
                out=w_codes[:, cols].bitcast(FP8X4),
                scales=w_scales[:, cols],
                in_=w_grouped[:, cols, :].rearrange("p n t -> p (n t)"),
            )

        x_grouped = keep.tile([P, S, PACK], BF16, name="x_grouped", align_bytes=64)
        x_codes = keep.tile([P, S], U32, name="x_codes", align_bytes=64)
        x_scales = keep.tile([P, S], U8, name="x_scales", align_bytes=64)

        banks = [1, 0, 7, 6, 5, 4, 3, 2, 1, 0]
        x_got = keep.tile([P, 2, S], F32, name="x_got")
        for t in range(2):
            nc.vector.tensor_copy(x_got[:, t, :], x_sb[t][:].indirect(offs_sb[:]))
        nc.scalar.copy(x_grouped[:, :, 0:2], x_got[:].rearrange("p t n -> p n t"))
        nc.vector.tensor_copy(x_grouped[:, :, 2], x_sb[2][:].indirect(offs_sb[:]))
        for s in range(X_SLICES):
            toks = slice(s * TOKENS, (s + 1) * TOKENS)
            entries = slice(s * TOKENS // LIST_ROWS, (s + 1) * TOKENS // LIST_ROWS)
            nc.vector.tensor_copy(x_grouped[:, toks, PACK - 1], x_sb[PACK - 1][:].indirect(offs_sb[:, entries]))
            if s + 1 < X_SLICES:
                nc.gpsimd.tensor_copy(
                    x_grouped[:, (s + 1) * TOKENS : (s + 1) * TOKENS + 2, PACK - 1],
                    x_grouped[:, s * TOKENS : s * TOKENS + 2, PACK - 1],
                )
            for c0 in (toks.start, toks.start + P):
                part = slice(c0, c0 + P)
                nc.vector.quantize_mx(
                    out=x_codes[:, part].bitcast(FP8X4),
                    scales=x_scales[:, part],
                    in_=x_grouped[:, part, :].rearrange("p n t -> p (n t)"),
                )
            for m in range(W_TILES):
                words = slice(m * P, (m + 1) * P)
                res = keep.tile([P, TOKENS], F32, name=f"res{s}_{m}")
                for c0 in range(0, TOKENS, P if m == 0 else TOKENS):
                    width = P if m == 0 else TOKENS
                    part = slice(toks.start + c0, toks.start + c0 + width)
                    acc = psum.tile([P, TOKENS], F32, name=f"acc{banks.pop()}")
                    nc.tensor.matmul_mx(
                        out=acc[:, 0:width],
                        lhsT=w_codes[:, words].bitcast(FP8X4),
                        lhsT_scale=w_scales[:, words],
                        rhs=x_codes[:, part].bitcast(FP8X4),
                        rhs_scale=x_scales[:, part],
                        start=True,
                        stop=True,
                    )
                    nc.scalar.activation(res[:, c0 : c0 + width], acc[:, 0:width], GELU, bias=b_sb[:, m : m + 1])
                nc.sync.dma_start(out[words, toks], res[:])
